import numpy as np
import ml_dtypes


def mxq(x, axis, fmt="e4m3"):
    dtype, down = {"e4m3": (ml_dtypes.float8_e4m3fn, 7), "e5m2": (ml_dtypes.float8_e5m2, 14)}[fmt]
    v = np.moveaxis(np.asarray(x, np.float32).astype(ml_dtypes.bfloat16).astype(np.float64), axis, -1)
    blocks = v.reshape(v.shape[:-1] + (-1, 32))
    amax = np.abs(blocks).max(-1, keepdims=True)
    byte = np.maximum(np.where(amax > 0, np.frexp(amax)[1] - 1 + 127, 0) - down, 1)
    scale = np.exp2(byte - 127.0)
    codes = (blocks / scale).astype(np.float32).astype(dtype).astype(np.float64)
    return np.moveaxis((codes * scale).reshape(v.shape), -1, axis)


WIDE = False


def mx_kscale(k):
    if not WIDE:
        return np.ones(k)
    levels = np.array([10, -10, 5, -5, 0])
    if k % 512:
        return np.exp2(np.random.permutation(np.resize(levels, k // 32))).repeat(32)
    a = np.empty((k // 512, 16))
    for p in range(k // 512):
        a[p, :8] = np.random.permutation(np.resize(levels, 8))
        for g in range(8):
            far = levels[np.abs(levels - a[p, g]) >= 10]
            a[p, g + 8] = far[np.random.randint(len(far))]
    return np.exp2(a.ravel()).repeat(32)


def f64(x):
    return np.asarray(x).astype(np.float64)


def striped(idx):
    return np.tile(idx.reshape(-1, 16).T, (8, 1)).astype(np.uint16)


def unstriped(offs):
    return offs[:16].T.reshape(-1).astype(np.int64)


def striped8(idx):
    return np.concatenate([x.reshape(-1, 16).T for x in idx]).astype(np.uint16)


def runs(offs, k):
    lists = np.stack([offs[16 * r : 16 * r + 16].T.reshape(-1) for r in range(8)]).astype(np.int64)
    return lists[np.arange(k) % 512 // 64]


def pack_weight(w):
    k, n = w.shape
    w = f64(np.asarray(w, np.float32).astype(ml_dtypes.bfloat16)).reshape(k // 32, 32, n)
    amax = np.abs(w).max(1)
    byte = np.clip(np.where(amax > 0, np.frexp(amax)[1] - 1 + 127 - 7, 1), 1, 254)
    scaled = (w * np.exp2(127.0 - byte)[:, None, :]).reshape(k, n).astype(np.float32)
    words = np.ascontiguousarray(scaled.reshape(k // 512, 128, 4, n).transpose(0, 1, 3, 2)).astype(ml_dtypes.float8_e4m3fn).view(np.uint8)
    return words, np.ascontiguousarray(byte.astype(np.uint8).reshape(k // 512, 16, n))


def unpack_weight(words, scales):
    g, p, n, _ = words.shape
    vals = np.ascontiguousarray(words).view(ml_dtypes.float8_e4m3fn).astype(np.float64) * np.repeat(np.exp2(scales.astype(np.float64) - 127.0), 8, axis=1)[..., None]
    return vals.transpose(0, 1, 3, 2).reshape(g * 512, n)


K, T, S, H, G, W = 512, 1024, 512, 512, 2048, 256


def setup_inputs():
    n = np.random.standard_normal
    s = mx_kscale(K)[:, None]
    packed_xT = pack_weight(n((K, T)) * s)
    packed_dT = pack_weight(n((K, G)) / s)
    perm = np.random.permutation(S)
    return {
        "x_words": packed_xT[0],
        "x_scales": packed_xT[1],
        "w1": (n((K, H)) / np.sqrt(K) / s).astype(np.float32),
        "gs": (np.random.uniform(0.5, 1.5, (K, 1)) * s).astype(np.float32),
        "d_words": packed_dT[0],
        "d_scales": packed_dT[1],
        "offs": striped(np.random.permutation(T)[:S]),
        "n1": striped8(np.stack([np.random.permutation(S) for _ in range(8)])),
        "n2": striped8(np.stack([np.random.permutation(S) for _ in range(8)])),
        "k1": striped8(np.random.randint(0, G, (8, H))),
        "k2": striped8(np.random.randint(0, G, (8, H))),
        "hz": striped8(np.random.randint(0, T, (8, S))),
        "n3": striped(perm[:W]),
        "n4": striped(perm[W:]),
    }


def reference(x_words, x_scales, w1, gs, d_words, d_scales, offs, n1, n2, k1, k2, hz, n3, n4):
    d_k1 = unpack_weight(d_words, d_scales)[np.arange(K)[:, None], runs(k1, K)]
    xq = unpack_weight(x_words, x_scales)[:, unstriped(offs)]
    y = mxq(f64(w1), 0, "e4m3").T @ xq
    ds = np.zeros((H, S))
    ds[np.arange(H)[:, None], runs(n1, H)] = y
    ds2 = np.zeros((H, S))
    ds2[np.arange(H)[:, None], runs(n2, H)] = y
    z = f64(gs) * np.maximum(ds, ds2)
    d_k2 = unpack_weight(d_words, d_scales)[np.arange(K)[:, None], runs(k2, K)]
    x_hz = unpack_weight(x_words, x_scales)[np.arange(K)[:, None], runs(hz, K)]
    h = 0.0625 * ((d_k1.T @ mxq(z, 0, "e4m3") + d_k2.T @ x_hz))
    pa = h[:, unstriped(n3)]
    pb = h[:, unstriped(n4)]
    ra = np.maximum(pa, pb)
    out = h.copy()
    out[:, unstriped(n3)] = ra
    return out

@@ -1,0 +1,162 @@
+from contextlib import ExitStack
+
+import concourse.mybir as mybir
+
+F32 = mybir.dt.float32
+BF16 = mybir.dt.bfloat16
+I32 = mybir.dt.int32
+U32 = mybir.dt.uint32
+U16 = mybir.dt.uint16
+U8 = mybir.dt.uint8
+FP8X4 = mybir.dt.float8_e4m3fn_x4
+COPY = mybir.ActivationFunctionType.Copy
+MAX = mybir.AluOpType.max
+
+P = 128
+K, T, S, H, G, W = 512, 1024, 512, 512, 2048, 256
+FLOPS = 3 * 2 * K * H * S
+
+
+def tile_picked_cmixhsendtwofill_none_p_kernel(
+    tc, x_words, x_scales, w1, gs, d_words, d_scales, offs, n1, n2, k1, k2, hz, n3, n4, out
+):
+    nc = tc.nc
+    with ExitStack() as ctx:
+        lists = ctx.enter_context(tc.tile_pool(name="lists", bufs=1))
+        sb = ctx.enter_context(tc.tile_pool(name="sb", bufs=1))
+        ps = ctx.enter_context(tc.psum_pool(name="ps", bufs=1))
+
+        def load_list(ap, name):
+            tile = lists.tile(list(ap.shape), U16, name=name)
+            nc.sync.dma_start(tile[:], ap)
+            return tile
+
+        x_bytes = sb.tile([P, T], U8, name="x_bytes")
+        d_bytes = sb.tile([P, G], U8, name="d_bytes")
+        nc.vector.memset(x_bytes[:].bitcast(I32), 0)
+        nc.vector.memset(d_bytes[:].bitcast(I32), 0)
+        x_planes = sb.tile([P, 2 * S], U8, name="x_planes", align_bytes=64)
+        d_planes = sb.tile([P, 2 * H], U8, name="d_planes", align_bytes=64)
+        nc.vector.memset(x_planes[:].bitcast(I32), 0)
+        nc.vector.memset(d_planes[:].bitcast(I32), 0)
+
+        offs_t = load_list(offs, "offs_t")
+        hz_t = load_list(hz, "hz_t")
+        k1_t = load_list(k1, "k1_t")
+        k2_t = load_list(k2, "k2_t")
+        nc.sync.dma_start(x_bytes[0:P:8, :].bitcast(I32), x_scales[0].bitcast(I32))
+        w_rows = w1.rearrange("(p j) c -> p j c", j=4)
+        w_raw = []
+        for half in range(2):
+            tile = sb.tile([P, 4, H // 2], F32, name=f"w_raw{half}")
+            nc.sync.dma_start(tile[:], w_rows[:, :, half * (H // 2) : (half + 1) * (H // 2)])
+            w_raw.append(tile)
+        x_tab = sb.tile([P, T], U32, name="x_tab")
+        nc.sync.dma_start(x_tab[:].bitcast(I32), x_words[0].rearrange("p n t -> p (n t)").bitcast(I32))
+        nc.sync.dma_start(d_bytes[0:P:8, :].bitcast(I32), d_scales[0].bitcast(I32))
+        n1_t = load_list(n1, "n1_t")
+        n2_t = load_list(n2, "n2_t")
+        gs_t = sb.tile([P, 4], F32, name="gs_t")
+        nc.sync.dma_start(gs_t[:], gs.rearrange("(p t) o -> p (t o)", t=4))
+        n3_t = load_list(n3, "n3_t")
+        n4_t = load_list(n4, "n4_t")
+
+        def place_rows(planes, picked):
+            for r in range(4):
+                nc.sync.dma_start(planes[r:P:32, :].bitcast(I32), picked[8 * r : P : 32, :].bitcast(I32))
+
+        x_picked = sb.tile([P, 2 * S], U8, name="x_picked")
+        nc.vector.tensor_copy(x_picked[:, 0:S], x_bytes[:].indirect(offs_t[:]))
+        nc.vector.tensor_copy(x_picked[:, S : 2 * S], x_bytes[:].indirect(hz_t[:]))
+        place_rows(x_planes, x_picked)
+        xq = sb.tile([P, S], U32, name="xq", align_bytes=64)
+        nc.vector.tensor_copy(xq[:], x_tab[:].indirect(offs_t[:]))
+
+        w_bf = sb.tile([P, 4, P, 4], BF16, name="w_bf", align_bytes=64)
+        for half in range(2):
+            nc.scalar.copy(
+                w_bf[:, :, half * 64 : (half + 1) * 64, :].rearrange("p t m j -> p m j t"),
+                w_raw[half][:].rearrange("p j (m t) -> p m j t", t=4),
+            )
+        d_tab = sb.tile([P, G], U32, name="d_tab", tag="w_raw1")
+        nc.sync.dma_start(d_tab[:].bitcast(I32), d_words[0].rearrange("p n t -> p (n t)").bitcast(I32))
+        w_codes = sb.tile([P, H], U32, name="w_codes", align_bytes=64)
+        w_scales = sb.tile([P, H], U8, name="w_scales", align_bytes=64)
+        nc.vector.quantize_mx(
+            out=w_codes[:].bitcast(FP8X4), scales=w_scales[:], in_=w_bf[:].rearrange("p t m j -> p (t m j)")
+        )
+        d_picked = sb.tile([P, 2 * H], U8, name="d_picked", tag="w_bf", align_bytes=64)
+        nc.vector.tensor_copy(d_picked[:, 0:H], d_bytes[:].indirect(k1_t[:]))
+        nc.vector.tensor_copy(d_picked[:, H : 2 * H], d_bytes[:].indirect(k2_t[:]))
+        place_rows(d_planes, d_picked)
+        xq_scales = x_planes[:, 0:S]
+        hz_scales = x_planes[:, S : 2 * S]
+        k1_scales = d_planes[:, 0:H]
+        k2_scales = d_planes[:, H : 2 * H]
+
+        z_bf = sb.tile([P, S, 4], BF16, name="z_bf", align_bytes=64)
+        for t in range(4):
+            cols = slice(t * P, (t + 1) * P)
+            y_ps = ps.tile([P, S], F32, name=f"y_ps{t}")
+            nc.tensor.matmul_mx(
+                out=y_ps[:], lhsT=w_codes[:, cols].bitcast(FP8X4), lhsT_scale=w_scales[:, cols],
+                rhs=xq[:].bitcast(FP8X4), rhs_scale=xq_scales, start=True, stop=True,
+            )
+            y = sb.tile([P, S], F32, name=f"y{t}", align_bytes=64)
+            nc.scalar.copy(y[:], y_ps[:])
+            ds = sb.tile([P, 2 * S], F32, name=f"ds{t}", align_bytes=64)
+            ds2 = sb.tile([P, 2 * S], F32, name=f"dt{t}", align_bytes=64)
+            nc.vector.tensor_copy(ds[:].indirect(n1_t[:]), y[:])
+            nc.vector.tensor_copy(ds2[:].indirect(n2_t[:]), y[:])
+            big = sb.tile([P, S], F32, name=f"big{t}")
+            nc.vector.tensor_tensor(big[:], ds[:, 0:S], ds2[:, 0:S], MAX)
+            nc.scalar.activation(z_bf[:, :, t], big[:], COPY, scale=gs_t[:, t : t + 1])
+
+        half_cols = H // 32
+        dk1 = []
+        dk2 = []
+        dk1.append(sb.tile([P, H // 2], U32, name="dk1a", tag="ds3", align_bytes=64))
+        nc.vector.tensor_copy(dk1[0][:], d_tab[:].indirect(k1_t[:, 0:half_cols]))
+        dk2.append(sb.tile([P, H // 2], U32, name="dk2a", tag="dt3", align_bytes=64))
+        nc.vector.tensor_copy(dk2[0][:], d_tab[:].indirect(k2_t[:, 0:half_cols]))
+        x_hz = sb.tile([P, S], U32, name="x_hz", tag="y3", align_bytes=64)
+        nc.vector.tensor_copy(x_hz[:], x_tab[:].indirect(hz_t[:]))
+        z_codes = sb.tile([P, S], U32, name="z_codes", align_bytes=64)
+        z_scales = sb.tile([P, S], U8, name="z_scales", align_bytes=64)
+        nc.vector.quantize_mx(
+            out=z_codes[:].bitcast(FP8X4), scales=z_scales[:], in_=z_bf[:].rearrange("p c t -> p (c t)")
+        )
+        late = sb.tile([P, H], U32, name="late", tag="z_bf", align_bytes=64)
+        nc.vector.tensor_copy(late[:, 0 : H // 2], d_tab[:].indirect(k1_t[:, half_cols : 2 * half_cols]))
+        nc.vector.tensor_copy(late[:, H // 2 : H], d_tab[:].indirect(k2_t[:, half_cols : 2 * half_cols]))
+        dk1_cols = [dk1[0][:, 0:P], dk1[0][:, P : 2 * P], late[:, 0:P], late[:, P : 2 * P]]
+        dk2_cols = [dk2[0][:, 0:P], dk2[0][:, P : 2 * P], late[:, 2 * P : 3 * P], late[:, 3 * P : 4 * P]]
+
+        hs = []
+        for i in range(4):
+            cols = slice(i * P, (i + 1) * P)
+            h_ps = ps.tile([P, S], F32, name=f"h_ps{i}")
+            nc.tensor.matmul_mx(
+                out=h_ps[:], lhsT=dk2_cols[i].bitcast(FP8X4), lhsT_scale=k2_scales[:, cols],
+                rhs=x_hz[:].bitcast(FP8X4), rhs_scale=hz_scales, start=True, stop=False,
+            )
+            nc.tensor.matmul_mx(
+                out=h_ps[:], lhsT=dk1_cols[i].bitcast(FP8X4), lhsT_scale=k1_scales[:, cols],
+                rhs=z_codes[:].bitcast(FP8X4), rhs_scale=z_scales[:], start=False, stop=True,
+            )
+            h = sb.tile([P, S], F32, name=f"h{i}")
+            nc.scalar.activation(h[:], h_ps[:], COPY, scale=0.0625)
+            hs.append(h)
+        for i in range(4):
+            h = hs[i]
+            pa = sb.tile([P, W], F32, name=f"pa{i}")
+            pb = sb.tile([P, W], F32, name=f"pb{i}")
+            nc.vector.tensor_copy(pa[:], h[:].indirect(n3_t[:]))
+            nc.vector.tensor_copy(pb[:], h[:].indirect(n4_t[:]))
+            ra = sb.tile([P, W], F32, name=f"ra{i}")
+            nc.vector.tensor_tensor(ra[:], pa[:], pb[:], MAX)
+            if i < 3:
+                nc.scalar.activation(h[:].indirect(n3_t[:]), ra[:], COPY)
+            else:
+                nc.vector.tensor_copy(h[:].indirect(n3_t[:]), ra[:])
+            nc.sync.dma_start(out[i * P : (i + 1) * P, :], h[:])

@@ -46,13 +46,11 @@ def tile_picked_cmixhsendtwofill_none_p_kernel(
         k2_t = load_list(k2, "k2_t")
         nc.sync.dma_start(x_bytes[0:P:8, :].bitcast(I32), x_scales[0].bitcast(I32))
         w_rows = w1.rearrange("(p j) c -> p j c", j=4)
-        w_raw = []
-        for half in range(2):
-            tile = sb.tile([P, 4, H // 2], F32, name=f"w_raw{half}")
-            nc.sync.dma_start(tile[:], w_rows[:, :, half * (H // 2) : (half + 1) * (H // 2)])
-            w_raw.append(tile)
+        w_raw = [sb.tile([P, 4, H // 2], F32, name=f"w_raw{c}") for c in range(2)]
         x_tab = sb.tile([P, T], U32, name="x_tab")
+        nc.sync.dma_start(w_raw[0][:], w_rows[:, :, 0 : H // 2])
         nc.sync.dma_start(x_tab[:].bitcast(I32), x_words[0].rearrange("p n t -> p (n t)").bitcast(I32))
+        nc.sync.dma_start(w_raw[1][:], w_rows[:, :, H // 2 : H])
         nc.sync.dma_start(d_bytes[0:P:8, :].bitcast(I32), d_scales[0].bitcast(I32))
         n1_t = load_list(n1, "n1_t")
         n2_t = load_list(n2, "n2_t")
@@ -71,12 +69,14 @@ def tile_picked_cmixhsendtwofill_none_p_kernel(
         place_rows(x_planes, x_picked)
         xq = sb.tile([P, S], U32, name="xq", align_bytes=64)
         nc.vector.tensor_copy(xq[:], x_tab[:].indirect(offs_t[:]))
+        x_hz = sb.tile([P, S], U32, name="x_hz", align_bytes=64)
+        nc.vector.tensor_copy(x_hz[:], x_tab[:].indirect(hz_t[:]))
 
         w_bf = sb.tile([P, 4, P, 4], BF16, name="w_bf", align_bytes=64)
-        for half in range(2):
+        for c in range(2):
             nc.scalar.copy(
-                w_bf[:, :, half * 64 : (half + 1) * 64, :].rearrange("p t m j -> p m j t"),
-                w_raw[half][:].rearrange("p j (m t) -> p m j t", t=4),
+                w_bf[:, :, c * 64 : (c + 1) * 64, :].rearrange("p t m j -> p m j t"),
+                w_raw[c][:].rearrange("p j (m t) -> p m j t", t=4),
             )
         d_tab = sb.tile([P, G], U32, name="d_tab", tag="w_raw1")
         nc.sync.dma_start(d_tab[:].bitcast(I32), d_words[0].rearrange("p n t -> p (n t)").bitcast(I32))
@@ -94,7 +94,7 @@ def tile_picked_cmixhsendtwofill_none_p_kernel(
         k1_scales = d_planes[:, 0:H]
         k2_scales = d_planes[:, H : 2 * H]
 
-        z_bf = sb.tile([P, S, 4], BF16, name="z_bf", align_bytes=64)
+        ys = []
         for t in range(4):
             cols = slice(t * P, (t + 1) * P)
             y_ps = ps.tile([P, S], F32, name=f"y_ps{t}")
@@ -104,59 +104,83 @@ def tile_picked_cmixhsendtwofill_none_p_kernel(
             )
             y = sb.tile([P, S], F32, name=f"y{t}", align_bytes=64)
             nc.scalar.copy(y[:], y_ps[:])
-            ds = sb.tile([P, 2 * S], F32, name=f"ds{t}", align_bytes=64)
-            ds2 = sb.tile([P, 2 * S], F32, name=f"dt{t}", align_bytes=64)
-            nc.vector.tensor_copy(ds[:].indirect(n1_t[:]), y[:])
-            nc.vector.tensor_copy(ds2[:].indirect(n2_t[:]), y[:])
-            big = sb.tile([P, S], F32, name=f"big{t}")
-            nc.vector.tensor_tensor(big[:], ds[:, 0:S], ds2[:, 0:S], MAX)
-            nc.scalar.activation(z_bf[:, :, t], big[:], COPY, scale=gs_t[:, t : t + 1])
+            ys.append(y)
 
-        half_cols = H // 32
-        dk1 = []
-        dk2 = []
-        dk1.append(sb.tile([P, H // 2], U32, name="dk1a", tag="ds3", align_bytes=64))
-        nc.vector.tensor_copy(dk1[0][:], d_tab[:].indirect(k1_t[:, 0:half_cols]))
-        dk2.append(sb.tile([P, H // 2], U32, name="dk2a", tag="dt3", align_bytes=64))
-        nc.vector.tensor_copy(dk2[0][:], d_tab[:].indirect(k2_t[:, 0:half_cols]))
-        x_hz = sb.tile([P, S], U32, name="x_hz", tag="y3", align_bytes=64)
-        nc.vector.tensor_copy(x_hz[:], x_tab[:].indirect(hz_t[:]))
-        z_codes = sb.tile([P, S], U32, name="z_codes", align_bytes=64)
-        z_scales = sb.tile([P, S], U8, name="z_scales", align_bytes=64)
-        nc.vector.quantize_mx(
-            out=z_codes[:].bitcast(FP8X4), scales=z_scales[:], in_=z_bf[:].rearrange("p c t -> p (c t)")
-        )
-        late = sb.tile([P, H], U32, name="late", tag="z_bf", align_bytes=64)
-        nc.vector.tensor_copy(late[:, 0 : H // 2], d_tab[:].indirect(k1_t[:, half_cols : 2 * half_cols]))
-        nc.vector.tensor_copy(late[:, H // 2 : H], d_tab[:].indirect(k2_t[:, half_cols : 2 * half_cols]))
-        dk1_cols = [dk1[0][:, 0:P], dk1[0][:, P : 2 * P], late[:, 0:P], late[:, P : 2 * P]]
-        dk2_cols = [dk2[0][:, 0:P], dk2[0][:, P : 2 * P], late[:, 2 * P : 3 * P], late[:, 3 * P : 4 * P]]
+        half = S // 2
+        halves = [slice(0, half), slice(half, S)]
+        z_bf = [sb.tile([P, half, 4], BF16, name=f"z_bf{u}", align_bytes=64) for u in range(2)]
+        ds = [sb.tile([P, 2 * S], F32, name=f"ds{t}") for t in range(4)]
+        ds2 = [sb.tile([P, 2 * S], F32, name=f"ds2{t}") for t in range(4)]
 
-        hs = []
+        def weigh(t, u, larger):
+            nc.scalar.activation(z_bf[u][:, :, t], larger, COPY, scale=gs_t[:, t : t + 1])
+
+        nc.vector.tensor_copy(ds[0][:].indirect(n1_t[:]), ys[0][:])
+        for t in range(3):
+            nc.vector.tensor_copy(ds2[t][:].indirect(n2_t[:]), ys[t][:])
+            nc.vector.tensor_copy(ds[t + 1][:].indirect(n1_t[:]), ys[t + 1][:])
+            larger = sb.tile([P, S], F32, name=f"larger{t}")
+            nc.vector.tensor_tensor(larger[:], ds[t][:, 0:S], ds2[t][:, 0:S], MAX)
+            for u in range(2):
+                weigh(t, u, larger[:, halves[u]])
+        nc.vector.tensor_copy(ds2[3][:].indirect(n2_t[:]), ys[3][:])
+        for u in range(2):
+            last = sb.tile([P, half], F32, name=f"last{u}", align_bytes=64)
+            nc.vector.tensor_tensor(last[:], ds[3][:, halves[u]], ds2[3][:, halves[u]], MAX)
+            weigh(3, u, last[:])
+
+        list_halves = [slice(0, H // 32), slice(H // 32, H // 16)]
+        dk2_lo = sb.tile([P, H // 2], U32, name="dk2_lo", align_bytes=64)
+        nc.vector.tensor_copy(dk2_lo[:], d_tab[:].indirect(k2_t[:, list_halves[0]]))
+        mid = sb.tile([P, H], U32, name="mid", tag="y3", align_bytes=64)
+        nc.vector.tensor_copy(mid[:, 0 : H // 2], d_tab[:].indirect(k2_t[:, list_halves[1]]))
+        nc.vector.tensor_copy(mid[:, H // 2 : H], d_tab[:].indirect(k1_t[:, list_halves[0]]))
+        z_codes = []
+        z_scales = []
+        for u in range(2):
+            codes = sb.tile([P, half], U32, name=f"z_codes{u}", align_bytes=64)
+            scales = sb.tile([P, half], U8, name=f"z_scales{u}", align_bytes=64)
+            nc.vector.quantize_mx(
+                out=codes[:].bitcast(FP8X4), scales=scales[:], in_=z_bf[u][:].rearrange("p c t -> p (c t)")
+            )
+            z_codes.append(codes)
+            z_scales.append(scales)
+        dk1_hi = sb.tile([P, H // 2], U32, name="dk1_hi", tag="last1", align_bytes=64)
+        nc.vector.tensor_copy(dk1_hi[:], d_tab[:].indirect(k1_t[:, list_halves[1]]))
+        dk1_cols = [mid[:, 2 * P : 3 * P], mid[:, 3 * P : 4 * P], dk1_hi[:, 0:P], dk1_hi[:, P : 2 * P]]
+        dk2_cols = [dk2_lo[:, 0:P], dk2_lo[:, P : 2 * P], mid[:, 0:P], mid[:, P : 2 * P]]
+
+        h_ps = [ps.tile([P, S], F32, name=f"h_ps{i}") for i in range(4)]
         for i in range(4):
-            cols = slice(i * P, (i + 1) * P)
-            h_ps = ps.tile([P, S], F32, name=f"h_ps{i}")
             nc.tensor.matmul_mx(
-                out=h_ps[:], lhsT=dk2_cols[i].bitcast(FP8X4), lhsT_scale=k2_scales[:, cols],
+                out=h_ps[i][:], lhsT=dk2_cols[i].bitcast(FP8X4), lhsT_scale=k2_scales[:, i * P : (i + 1) * P],
                 rhs=x_hz[:].bitcast(FP8X4), rhs_scale=hz_scales, start=True, stop=False,
             )
-            nc.tensor.matmul_mx(
-                out=h_ps[:], lhsT=dk1_cols[i].bitcast(FP8X4), lhsT_scale=k1_scales[:, cols],
-                rhs=z_codes[:].bitcast(FP8X4), rhs_scale=z_scales[:], start=False, stop=True,
-            )
-            h = sb.tile([P, S], F32, name=f"h{i}")
-            nc.scalar.activation(h[:], h_ps[:], COPY, scale=0.0625)
-            hs.append(h)
+        hs = []
         for i in range(4):
-            h = hs[i]
-            pa = sb.tile([P, W], F32, name=f"pa{i}")
-            pb = sb.tile([P, W], F32, name=f"pb{i}")
-            nc.vector.tensor_copy(pa[:], h[:].indirect(n3_t[:]))
-            nc.vector.tensor_copy(pb[:], h[:].indirect(n4_t[:]))
-            ra = sb.tile([P, W], F32, name=f"ra{i}")
-            nc.vector.tensor_tensor(ra[:], pa[:], pb[:], MAX)
-            if i < 3:
-                nc.scalar.activation(h[:].indirect(n3_t[:]), ra[:], COPY)
-            else:
-                nc.vector.tensor_copy(h[:].indirect(n3_t[:]), ra[:])
-            nc.sync.dma_start(out[i * P : (i + 1) * P, :], h[:])
+            for u in range(2):
+                nc.tensor.matmul_mx(
+                    out=h_ps[i][:, halves[u]], lhsT=dk1_cols[i].bitcast(FP8X4),
+                    lhsT_scale=k1_scales[:, i * P : (i + 1) * P],
+                    rhs=z_codes[u][:].bitcast(FP8X4), rhs_scale=z_scales[u][:], start=False, stop=(u == 1),
+                )
+            h = sb.tile([P, S], F32, name=f"h{i}")
+            nc.scalar.activation(h[:], h_ps[i][:], COPY, scale=0.0625)
+            hs.append(h)
+
+        pa = sb.tile([P, 4, W], F32, name="pa")
+        pb = sb.tile([P, 4, W], F32, name="pb")
+        ra = sb.tile([P, 4, W], F32, name="ra")
+        nc.scalar.activation(pa[:, 3, :], hs[3][:].indirect(n3_t[:]), COPY)
+        nc.scalar.activation(pb[:, 3, :], hs[3][:].indirect(n4_t[:]), COPY)
+        for i in range(3):
+            nc.vector.tensor_copy(pa[:, i, :], hs[i][:].indirect(n3_t[:]))
+            nc.vector.tensor_copy(pb[:, i, :], hs[i][:].indirect(n4_t[:]))
+            tiles = slice(i, i + 1) if i < 2 else slice(2, 4)
+            nc.vector.tensor_tensor(ra[:, tiles, :], pa[:, tiles, :], pb[:, tiles, :], MAX)
+        for i in (0, 1, 3):
+            nc.scalar.activation(hs[i][:].indirect(n3_t[:]), ra[:, i, :], COPY)
+        nc.vector.tensor_copy(hs[2][:].indirect(n3_t[:]), ra[:, 2, :])
+        for i in range(3):
+            nc.sync.dma_start(out[i * P : (i + 1) * P, :], hs[i][:])
+        nc.scalar.dma_start(out[3 * P : 4 * P, :], hs[3][:])

from contextlib import ExitStack

import concourse.mybir as mybir

F32 = mybir.dt.float32
BF16 = mybir.dt.bfloat16
I32 = mybir.dt.int32
U32 = mybir.dt.uint32
U16 = mybir.dt.uint16
U8 = mybir.dt.uint8
FP8X4 = mybir.dt.float8_e4m3fn_x4
COPY = mybir.ActivationFunctionType.Copy
MAX = mybir.AluOpType.max

P = 128
K, T, S, H, G, W = 512, 1024, 512, 512, 2048, 256
FLOPS = 3 * 2 * K * H * S


def tile_picked_cmixhsendtwofill_none_p_kernel(
    tc, x_words, x_scales, w1, gs, d_words, d_scales, offs, n1, n2, k1, k2, hz, n3, n4, out
):
    nc = tc.nc
    with ExitStack() as ctx:
        lists = ctx.enter_context(tc.tile_pool(name="lists", bufs=1))
        sb = ctx.enter_context(tc.tile_pool(name="sb", bufs=1))
        ps = ctx.enter_context(tc.psum_pool(name="ps", bufs=1))

        def load_list(ap, name):
            tile = lists.tile(list(ap.shape), U16, name=name)
            nc.sync.dma_start(tile[:], ap)
            return tile

        x_bytes = sb.tile([P, T], U8, name="x_bytes")
        d_bytes = sb.tile([P, G], U8, name="d_bytes")
        nc.vector.memset(x_bytes[:].bitcast(I32), 0)
        nc.vector.memset(d_bytes[:].bitcast(I32), 0)
        x_planes = sb.tile([P, 2 * S], U8, name="x_planes", align_bytes=64)
        d_planes = sb.tile([P, 2 * H], U8, name="d_planes", align_bytes=64)
        nc.vector.memset(x_planes[:].bitcast(I32), 0)
        nc.vector.memset(d_planes[:].bitcast(I32), 0)

        offs_t = load_list(offs, "offs_t")
        hz_t = load_list(hz, "hz_t")
        k1_t = load_list(k1, "k1_t")
        k2_t = load_list(k2, "k2_t")
        nc.sync.dma_start(x_bytes[0:P:8, :].bitcast(I32), x_scales[0].bitcast(I32))
        w_rows = w1.rearrange("(p j) c -> p j c", j=4)
        w_raw = [sb.tile([P, 4, H // 2], F32, name=f"w_raw{c}") for c in range(2)]
        x_tab = sb.tile([P, T], U32, name="x_tab")
        nc.sync.dma_start(w_raw[0][:], w_rows[:, :, 0 : H // 2])
        nc.sync.dma_start(x_tab[:].bitcast(I32), x_words[0].rearrange("p n t -> p (n t)").bitcast(I32))
        nc.sync.dma_start(w_raw[1][:], w_rows[:, :, H // 2 : H])
        nc.sync.dma_start(d_bytes[0:P:8, :].bitcast(I32), d_scales[0].bitcast(I32))
        n1_t = load_list(n1, "n1_t")
        n2_t = load_list(n2, "n2_t")
        gs_t = sb.tile([P, 4], F32, name="gs_t")
        nc.sync.dma_start(gs_t[:], gs.rearrange("(p t) o -> p (t o)", t=4))
        n3_t = load_list(n3, "n3_t")
        n4_t = load_list(n4, "n4_t")

        def place_rows(planes, picked):
            for r in range(4):
                nc.sync.dma_start(planes[r:P:32, :].bitcast(I32), picked[8 * r : P : 32, :].bitcast(I32))

        x_picked = sb.tile([P, 2 * S], U8, name="x_picked")
        nc.vector.tensor_copy(x_picked[:, 0:S], x_bytes[:].indirect(offs_t[:]))
        nc.vector.tensor_copy(x_picked[:, S : 2 * S], x_bytes[:].indirect(hz_t[:]))
        place_rows(x_planes, x_picked)
        xq = sb.tile([P, S], U32, name="xq", align_bytes=64)
        nc.vector.tensor_copy(xq[:], x_tab[:].indirect(offs_t[:]))
        x_hz = sb.tile([P, S], U32, name="x_hz", align_bytes=64)
        nc.vector.tensor_copy(x_hz[:], x_tab[:].indirect(hz_t[:]))

        w_bf = sb.tile([P, 4, P, 4], BF16, name="w_bf", align_bytes=64)
        for c in range(2):
            nc.scalar.copy(
                w_bf[:, :, c * 64 : (c + 1) * 64, :].rearrange("p t m j -> p m j t"),
                w_raw[c][:].rearrange("p j (m t) -> p m j t", t=4),
            )
        d_tab = sb.tile([P, G], U32, name="d_tab", tag="w_raw1")
        nc.sync.dma_start(d_tab[:].bitcast(I32), d_words[0].rearrange("p n t -> p (n t)").bitcast(I32))
        w_codes = sb.tile([P, H], U32, name="w_codes", align_bytes=64)
        w_scales = sb.tile([P, H], U8, name="w_scales", align_bytes=64)
        nc.vector.quantize_mx(
            out=w_codes[:].bitcast(FP8X4), scales=w_scales[:], in_=w_bf[:].rearrange("p t m j -> p (t m j)")
        )
        d_picked = sb.tile([P, 2 * H], U8, name="d_picked", tag="w_bf", align_bytes=64)
        nc.vector.tensor_copy(d_picked[:, 0:H], d_bytes[:].indirect(k1_t[:]))
        nc.vector.tensor_copy(d_picked[:, H : 2 * H], d_bytes[:].indirect(k2_t[:]))
        place_rows(d_planes, d_picked)
        xq_scales = x_planes[:, 0:S]
        hz_scales = x_planes[:, S : 2 * S]
        k1_scales = d_planes[:, 0:H]
        k2_scales = d_planes[:, H : 2 * H]

        ys = []
        for t in range(4):
            cols = slice(t * P, (t + 1) * P)
            y_ps = ps.tile([P, S], F32, name=f"y_ps{t}")
            nc.tensor.matmul_mx(
                out=y_ps[:], lhsT=w_codes[:, cols].bitcast(FP8X4), lhsT_scale=w_scales[:, cols],
                rhs=xq[:].bitcast(FP8X4), rhs_scale=xq_scales, start=True, stop=True,
            )
            y = sb.tile([P, S], F32, name=f"y{t}", align_bytes=64)
            nc.scalar.copy(y[:], y_ps[:])
            ys.append(y)

        half = S // 2
        halves = [slice(0, half), slice(half, S)]
        z_bf = [sb.tile([P, half, 4], BF16, name=f"z_bf{u}", align_bytes=64) for u in range(2)]
        ds = [sb.tile([P, 2 * S], F32, name=f"ds{t}") for t in range(4)]
        ds2 = [sb.tile([P, 2 * S], F32, name=f"ds2{t}") for t in range(4)]

        def weigh(t, u, larger):
            nc.scalar.activation(z_bf[u][:, :, t], larger, COPY, scale=gs_t[:, t : t + 1])

        nc.vector.tensor_copy(ds[0][:].indirect(n1_t[:]), ys[0][:])
        for t in range(3):
            nc.vector.tensor_copy(ds2[t][:].indirect(n2_t[:]), ys[t][:])
            nc.vector.tensor_copy(ds[t + 1][:].indirect(n1_t[:]), ys[t + 1][:])
            larger = sb.tile([P, S], F32, name=f"larger{t}")
            nc.vector.tensor_tensor(larger[:], ds[t][:, 0:S], ds2[t][:, 0:S], MAX)
            for u in range(2):
                weigh(t, u, larger[:, halves[u]])
        nc.vector.tensor_copy(ds2[3][:].indirect(n2_t[:]), ys[3][:])
        for u in range(2):
            last = sb.tile([P, half], F32, name=f"last{u}", align_bytes=64)
            nc.vector.tensor_tensor(last[:], ds[3][:, halves[u]], ds2[3][:, halves[u]], MAX)
            weigh(3, u, last[:])

        list_halves = [slice(0, H // 32), slice(H // 32, H // 16)]
        dk2_lo = sb.tile([P, H // 2], U32, name="dk2_lo", align_bytes=64)
        nc.vector.tensor_copy(dk2_lo[:], d_tab[:].indirect(k2_t[:, list_halves[0]]))
        mid = sb.tile([P, H], U32, name="mid", tag="y3", align_bytes=64)
        nc.vector.tensor_copy(mid[:, 0 : H // 2], d_tab[:].indirect(k2_t[:, list_halves[1]]))
        nc.vector.tensor_copy(mid[:, H // 2 : H], d_tab[:].indirect(k1_t[:, list_halves[0]]))
        z_codes = []
        z_scales = []
        for u in range(2):
            codes = sb.tile([P, half], U32, name=f"z_codes{u}", align_bytes=64)
            scales = sb.tile([P, half], U8, name=f"z_scales{u}", align_bytes=64)
            nc.vector.quantize_mx(
                out=codes[:].bitcast(FP8X4), scales=scales[:], in_=z_bf[u][:].rearrange("p c t -> p (c t)")
            )
            z_codes.append(codes)
            z_scales.append(scales)
        dk1_hi = sb.tile([P, H // 2], U32, name="dk1_hi", tag="last1", align_bytes=64)
        nc.vector.tensor_copy(dk1_hi[:], d_tab[:].indirect(k1_t[:, list_halves[1]]))
        dk1_cols = [mid[:, 2 * P : 3 * P], mid[:, 3 * P : 4 * P], dk1_hi[:, 0:P], dk1_hi[:, P : 2 * P]]
        dk2_cols = [dk2_lo[:, 0:P], dk2_lo[:, P : 2 * P], mid[:, 0:P], mid[:, P : 2 * P]]

        h_ps = [ps.tile([P, S], F32, name=f"h_ps{i}") for i in range(4)]
        for i in range(4):
            nc.tensor.matmul_mx(
                out=h_ps[i][:], lhsT=dk2_cols[i].bitcast(FP8X4), lhsT_scale=k2_scales[:, i * P : (i + 1) * P],
                rhs=x_hz[:].bitcast(FP8X4), rhs_scale=hz_scales, start=True, stop=False,
            )
        hs = []
        for i in range(4):
            for u in range(2):
                nc.tensor.matmul_mx(
                    out=h_ps[i][:, halves[u]], lhsT=dk1_cols[i].bitcast(FP8X4),
                    lhsT_scale=k1_scales[:, i * P : (i + 1) * P],
                    rhs=z_codes[u][:].bitcast(FP8X4), rhs_scale=z_scales[u][:], start=False, stop=(u == 1),
                )
            h = sb.tile([P, S], F32, name=f"h{i}")
            nc.scalar.activation(h[:], h_ps[i][:], COPY, scale=0.0625)
            hs.append(h)

        pa = sb.tile([P, 4, W], F32, name="pa")
        pb = sb.tile([P, 4, W], F32, name="pb")
        ra = sb.tile([P, 4, W], F32, name="ra")
        nc.scalar.activation(pa[:, 3, :], hs[3][:].indirect(n3_t[:]), COPY)
        nc.scalar.activation(pb[:, 3, :], hs[3][:].indirect(n4_t[:]), COPY)
        for i in range(3):
            nc.vector.tensor_copy(pa[:, i, :], hs[i][:].indirect(n3_t[:]))
            nc.vector.tensor_copy(pb[:, i, :], hs[i][:].indirect(n4_t[:]))
            tiles = slice(i, i + 1) if i < 2 else slice(2, 4)
            nc.vector.tensor_tensor(ra[:, tiles, :], pa[:, tiles, :], pb[:, tiles, :], MAX)
        for i in (0, 1, 3):
            nc.scalar.activation(hs[i][:].indirect(n3_t[:]), ra[:, i, :], COPY)
        nc.vector.tensor_copy(hs[2][:].indirect(n3_t[:]), ra[:, 2, :])
        for i in range(3):
            nc.sync.dma_start(out[i * P : (i + 1) * P, :], hs[i][:])
        nc.scalar.dma_start(out[3 * P : 4 * P, :], hs[3][:])
